import numpy as np
import ml_dtypes


def mxq(x, axis, fmt="e4m3"):
    dtype, down = {"e4m3": (ml_dtypes.float8_e4m3fn, 7), "e5m2": (ml_dtypes.float8_e5m2, 14)}[fmt]
    v = np.moveaxis(np.asarray(x, np.float32).astype(ml_dtypes.bfloat16).astype(np.float64), axis, -1)
    blocks = v.reshape(v.shape[:-1] + (-1, 32))
    amax = np.abs(blocks).max(-1, keepdims=True)
    byte = np.maximum(np.where(amax > 0, np.frexp(amax)[1] - 1 + 127, 0) - down, 1)
    scale = np.exp2(byte - 127.0)
    codes = (blocks / scale).astype(np.float32).astype(dtype).astype(np.float64)
    return np.moveaxis((codes * scale).reshape(v.shape), -1, axis)


WIDE = False


def mx_kscale(k):
    if not WIDE:
        return np.ones(k)
    levels = np.array([10, -10, 5, -5, 0])
    if k % 512:
        return np.exp2(np.random.permutation(np.resize(levels, k // 32))).repeat(32)
    a = np.empty((k // 512, 16))
    for p in range(k // 512):
        a[p, :8] = np.random.permutation(np.resize(levels, 8))
        for g in range(8):
            far = levels[np.abs(levels - a[p, g]) >= 10]
            a[p, g + 8] = far[np.random.randint(len(far))]
    return np.exp2(a.ravel()).repeat(32)


BF16 = ml_dtypes.bfloat16


def bf(x):
    return np.asarray(x, np.float32).astype(BF16)


def f64(x):
    return np.asarray(x).astype(np.float64)

def planes(Y):
    n, m = Y.shape
    b = f64(bf(Y)).reshape(n // 32, 32, m)
    amax = np.abs(b).max(1)
    byte = np.clip(np.where(amax > 0, np.frexp(amax)[1] - 1 + 127 - 7, 1), 1, 254)
    codes = (b * np.exp2(127.0 - byte)[:, None, :]).reshape(n, m).astype(np.float32).astype(ml_dtypes.float8_e4m3fn).view(np.uint8)
    words = codes.reshape(n // 512, 128, 4, m).transpose(0, 1, 3, 2)
    return np.ascontiguousarray(words), np.ascontiguousarray(byte.astype(np.uint8).reshape(n // 512, 16, m))


S, B, D, R = 1024, 2, 1536, 512

GELU_C = 0.7978845608028654


def setup_inputs():
    s = mx_kscale(S)
    t = mx_kscale(R)
    f = np.exp(0.8 * np.random.randn(D))
    x = np.random.randn(S, B, D) * s[:, None, None]
    w_down = np.random.randn(S, R) / np.sqrt(S) / s[:, None]
    slot_scale = (1.0 + 0.1 * np.random.randn(R)) * t
    w_up = np.random.randn(R, S) / np.sqrt(R) / t[:, None]
    b_up = 0.3 * np.random.randn(S)
    gain = f * (1.0 + 0.1 * np.random.randn(D))
    resid = f * np.random.randn(S, B, D)
    return {"x": bf(x), "w_down": bf(w_down), "slot_scale": bf(slot_scale), "w_up": bf(w_up),
            "b_up": bf(b_up), "gain": bf(gain), "resid": bf(resid)}


def reference(x, w_down, slot_scale, w_up, b_up, gain, resid):
    X = f64(x).reshape(S, B * D)
    z = mxq(f64(w_down), 0, "e4m3").T @ mxq(X, 0, "e4m3")
    h = 0.5 * z * (1.0 + np.tanh(GELU_C * (z + 0.044715 * z * z * z)))
    h = h * f64(slot_scale)[:, None]
    u = mxq(f64(w_up), 0, "e4m3").T @ mxq(h, 0, "e4m3")
    y = f64(resid) + f64(gain) * (u.reshape(S, B, D) + f64(b_up)[:, None, None])
    Y = y.reshape(S * B, D).T
    words, scales = planes(Y)
    return y, words, scales

from contextlib import ExitStack

import concourse.mybir as mybir
from concourse.masks import make_identity

S, B, D, R = 1024, 2, 1536, 512
FLOPS = 2 * 2 * S * R * B * D

F32 = mybir.dt.float32
BF16 = mybir.dt.bfloat16
U32 = mybir.dt.uint32
I32 = mybir.dt.int32
U8 = mybir.dt.uint8
FP8X4 = mybir.dt.float8_e4m3fn_x4
GELU = mybir.ActivationFunctionType.Gelu_apprx_tanh
ADD = mybir.AluOpType.add
MULT = mybir.AluOpType.mult

P = 128
PACK = 4
PASSES = 2
G = 512
GROUPS = D // G
TILES = S // P
CH = 128
UNITS = GROUPS * TILES


BUFS = {
    "gain": 2, "wd_raw": 2, "wu_raw": 2, "x_raw": 8, "r": 8, "w_grp": 3, "x_grp": 6, "x_codes": 3, "x_scales": 3,
    "z": 2, "act": 3, "h": 3, "h_codes": 2, "h_scales": 2, "u": 3, "y": 10, "y16": 4, "yt": 2, "y_grp": 5,
    "y_codes": 2, "y_scales": 2,
}
POOL_COLS = (512, 320)
DEFER = (4, 8, 11)
DOUBLE = (18, 21, 22)
P1_DVE = ()
LATE = 32
QLAG = 4


def program_order():
    order = []
    add = lambda *step: order.append(step)
    add("load_small")
    add("load_wd", 0)
    add("load_x", 0, 0, 0)
    add("load_wd", 1)
    add("load_x", 0, 0, 1)
    add("load_x", 0, 1, 0)
    add("load_x", 0, 1, 1)
    add("load_wu", 0)
    add("load_wu", 1)
    add("load_x", 1, 0, 0)
    add("load_x", 1, 0, 1)
    add("load_gain", 0)
    add("load_r", 0)
    add("load_r", 1)
    add("load_x", 1, 1, 0)
    add("load_x", 1, 1, 1)
    for k in range(2, 6):
        add("load_r", k)
    add("setup")
    add("spread_scale")
    add("bias_rows")
    add("bias_turn")
    add("group_wd", 0, "dve")
    add("bias_cols")
    add("quant_wd", 0)
    for n in range(4):
        add("group_x", n, 0, "act")
    add("group_wd", 1, "dve")
    add("group_x", 0, 1, "act")
    add("group_x", 1, 1, "act")
    add("group_x", 2, 1, "dve")
    add("quant_wd", 1)
    add("quant_x", 0)
    add("down", 0)
    add("group_x", 3, 1, "dve")
    add("group_x", 4, 0, "act")
    add("group_x", 5, 0, "act")
    add("quant_x", 1)
    add("down", 1)
    for i in range(9):
        if i != 7:
            add("gelu", i)
        if i == 8:
            add("quant_h", 7)
            add("up", 0, 1)
        if 2 <= i + 2 < 4:
            add("quant_x", i + 2)
            add("down", i + 2)
        if i + 4 < 8:
            add("group_x", i + 4, 1, "dve")
        if i + 6 < 8:
            add("group_x", i + 6, 0, "act")
        if 2 <= i < 4:
            add("group_wu", 0, i % 2, "act")
        if i in (4, 5):
            add("group_wu", 1, i % 2, "dve")
        if i in (4, 5, 7):
            add("group_x", {4: 8, 5: 9, 7: 10}[i], 0, "act")
            add("group_x", {4: 8, 5: 9, 7: 10}[i], 1, "act")
        if i == 7:
            continue
        if i == 6:
            add("scale_h", 5)
            add("quant_h", 4)
            add("quant_x", 8)
            add("down", 8)
            add("quant_h", 5)
            add("scale_h", 6)
            add("quant_wu", 1)
            add("gelu", 7)
            add("quant_h", 6)
            add("scale_h", 7)
            add("quant_x", 9)
            add("up", 0, 0)
            add("down", 9)
            continue
        if i == 8:
            continue
        if i >= 2:
            add("quant_h", i - 2)
        if i >= 1:
            add("scale_h", i - 1)
        if 4 <= i + 2 < 10:
            add("quant_x", i + 2)
            add("down", i + 2)
        if i == 5:
            add("quant_wu", 0)
    rounds = {}
    m = 0
    for k in range(2, UNITS + 2):
        count = 0 if k in DEFER else 1
        if k in DOUBLE:
            count = 2
        rounds[k] = list(range(m, m + count))
        m += len(rounds[k])
    for k in range(UNITS + 6):
        pool_cols = POOL_COLS[0] if k + 8 < UNITS else POOL_COLS[1]
        if k == UNITS:
            pool_cols = 0
        late = LATE if POOL_COLS[0] else 0
        split = G - pool_cols // 2
        for m in rounds.get(k - 1, []):
            add("turn_y", m)
        if late and 1 <= k < UNITS:
            add("affine", k - 1, 1, G - late, G)
            add("add_r", k - 1, split, G, "pool")
        for m in rounds.get(k - QLAG, []):
            add("quant_y", m)
            g, j = divmod(m, TILES)
            if j % 2 == 1:
                add("store_codes", g, j - 1, j + 1)
            if j == TILES - 1:
                add("store_scales", g)
        if k < UNITS:
            add("affine", k, 0, 0, G)
            add("affine", k, 1, 0, G - late if k < UNITS - 1 else G)
        if k + 9 < UNITS:
            add("gelu", k + 9)
        if k + 8 < UNITS:
            add("scale_h", k + 8)
        for m in rounds.get(k, []):
            add("round_y", m, "act")
        if k + 10 < UNITS:
            add("quant_x", k + 10)
        if k + 8 < UNITS:
            add("quant_h", k + 8)
        if k + 1 < UNITS:
            add("up", k + 1, 0)
            add("up", k + 1, 1)
        if k + 10 < UNITS:
            add("down", k + 10)
        for m in rounds.get(k - 1, []):
            add("group_y", m, "act")
        if 1 <= k <= UNITS:
            add("add_r", k - 1, 0, split, "dve")
            add("store_y", k - 1)
        if k + 11 < UNITS:
            add("group_x", k + 11, 0, "act")
            add("group_x", k + 11, 1, "dve" if k in P1_DVE else "act")
        if k + 6 < UNITS:
            add("load_r", k + 6)
        if k < 4:
            add("load_x", 2, k // 2, k % 2)
        if k in (3, 11):
            add("load_gain", k // 8 + 1)
    assert sum(s[0] == "quant_y" for s in order) == UNITS
    return order


def tile_sequence_bottleneck_adapter_h3_kernel(
    tc, x, w_down, slot_scale, w_up, b_up, gain, resid, out_0, out_1, out_2
):
    nc = tc.nc
    x_rows = x.rearrange("(a p j) b d -> a p j b d", p=P, j=PACK)
    wd_rows = w_down.rearrange("(a p j) r -> a p j r", p=P, j=PACK)
    wu_rows = w_up.rearrange("(p j) s -> p j s", j=PACK)

    with ExitStack() as ctx:
        keep = ctx.enter_context(tc.tile_pool(name="keep", bufs=1))
        work = ctx.enter_context(tc.tile_pool(name="work", bufs=1))
        psum = ctx.enter_context(tc.psum_pool(name="psum", bufs=1))
        ctx.enter_context(tc.manual_schedule())

        ident = keep.tile([P, P], F32, name="ident", align_bytes=64)
        b_rows = keep.tile([S // P, P], BF16, name="b_rows")
        b_square = keep.tile([P, P], F32, name="b_square", align_bytes=64)
        b_col = keep.tile([P, S // P], F32, name="b_col")
        scale_raw = keep.tile([P, PACK], BF16, name="scale_raw")
        scale_rep = keep.tile([P, P // PACK, PACK], F32, name="scale_rep", align_bytes=64)
        scale_turned = keep.tile([P, P], F32, name="scale_turned", align_bytes=64)
        scale_bank = psum.tile([P, CH * PACK], F32, name="scale_bank", tag="scale_bank", bufs=1)
        warm = keep.tile([P, 1], F32, name="warm")
        wd_codes = keep.tile([P, PASSES, R], U32, name="wd_codes", align_bytes=64)
        wd_scales = keep.tile([P, PASSES, R], U8, name="wd_scales", align_bytes=64)
        wu_codes = keep.tile([P, S], U32, name="wu_codes", align_bytes=64)
        wu_scales = keep.tile([P, S], U8, name="wu_scales", align_bytes=64)
        t = {}

        def new(pool, kind, key, shape, dtype):
            t[kind, key] = pool.tile(shape, dtype, name=kind, tag=kind, bufs=BUFS[kind], align_bytes=64)
            return t[kind, key]

        def new_bank(kind, key, shape):
            t[kind, key] = psum.tile(shape, F32, name=kind, tag=kind, bufs=BUFS[kind])
            return t[kind, key]

        def copy_on(engine, out, in_):
            if engine == "act":
                nc.scalar.copy(out=out, in_=in_)
            else:
                nc.vector.tensor_copy(out=out, in_=in_)

        def interleave(engine, dst, src):
            copy_on(
                engine,
                dst.rearrange("p (c i) t -> p c t i", i=4),
                src.rearrange("p t (c i) -> p c t i", i=4),
            )

        def setup():
            make_identity(nc, ident[:])
            nc.vector.memset(b_square[:], 0.0)
            nc.scalar.activation(out=warm[:], in_=b_square[:, 0:1], func=GELU)

        def load_small():
            nc.scalar.dma_start(out=scale_raw[:], in_=slot_scale.rearrange("(p t) -> p t", t=PACK))
            nc.scalar.dma_start(out=b_rows[:], in_=b_up.rearrange("(j p) -> j p", p=P))

        def spread_scale():
            nc.vector.tensor_copy(out=scale_rep[:], in_=scale_raw[:].unsqueeze(1).to_broadcast([P, P // PACK, PACK]))

        def bias_rows():
            nc.vector.tensor_copy(out=b_square[0 : S // P, :], in_=b_rows[:])

        def bias_turn():
            bank = new_bank("yt", "bias", [P, PACK, P])
            nc.tensor.transpose(bank[:, 0, :], b_square[:], ident[:])
            nc.tensor.transpose(bank[:, 1, :], scale_rep[:].rearrange("p c t -> p (c t)"), ident[:])

        def bias_cols():
            nc.vector.tensor_copy(out=b_col[:], in_=t["yt", "bias"][:, 0, 0 : S // P])
            nc.vector.tensor_copy(out=scale_turned[:], in_=t["yt", "bias"][:, 1, :])
            for q in range(PACK):
                nc.tensor.transpose(scale_bank[:, q * P : (q + 1) * P], scale_turned[:], ident[:])

        def load_gain(g):
            tile = new(work, "gain", g, [P, G], BF16)
            nc.sync.dma_start(out=tile[:], in_=gain[g * G : (g + 1) * G].partition_broadcast(P))

        def load_wd(a):
            tile = new(work, "wd_raw", a, [P, PACK, R], BF16)
            nc.sync.dma_start(out=tile[:], in_=wd_rows[a])

        def load_wu(h):
            tile = new(work, "wu_raw", h, [P, PACK, G], BF16)
            nc.sync.dma_start(out=tile[:], in_=wu_rows[:, :, h * G : (h + 1) * G])

        def load_x(g, b, a):
            tile = new(work, "x_raw", (g, b, a), [P, PACK, G], BF16)
            nc.sync.dma_start(out=tile[:], in_=x_rows[a, :, :, b, g * G : (g + 1) * G])

        def load_r(k):
            g, j = divmod(k, TILES)
            tile = new(work, "r", k, [P, B, G], BF16)
            nc.sync.dma_start(out=tile[:], in_=resid[j * P : (j + 1) * P, :, g * G : (g + 1) * G])

        def group_wd(a, engine):
            tile = new(work, "w_grp", ("wd", a), [P, R * PACK], BF16)
            copy_on(
                engine,
                tile[:].rearrange("p (t m j) -> p t m j", t=PACK, j=PACK),
                t["wd_raw", a][:].rearrange("p j (m t) -> p t m j", t=PACK),
            )

        def quant_wd(a):
            nc.vector.quantize_mx(
                out=wd_codes[:, a, :].bitcast(FP8X4), scales=wd_scales[:, a, :], in_=t["w_grp", ("wd", a)][:]
            )

        def group_wu(h, part, engine):
            if part == 0:
                new(work, "w_grp", ("wu", h), [P, G * PACK], BF16)
            half = G // 2
            dst = t["w_grp", ("wu", h)][:].rearrange("p (c t) -> p c t", t=PACK)
            cols = slice(part * half, (part + 1) * half)
            interleave(engine, dst[:, cols, :], t["wu_raw", h][:, :, cols])

        def quant_wu(h):
            cols = slice(h * G, (h + 1) * G)
            nc.vector.quantize_mx(
                out=wu_codes[:, cols].bitcast(FP8X4), scales=wu_scales[:, cols], in_=t["w_grp", ("wu", h)][:]
            )

        def group_x(n, a, engine):
            g, rest = divmod(n, TILES)
            b, c = divmod(rest, G // CH)
            if ("x_grp", n) not in t:
                new(work, "x_grp", n, [P, PASSES, CH, PACK], BF16)
            interleave(engine, t["x_grp", n][:, a, :, :], t["x_raw", (g, b, a)][:, :, c * CH : (c + 1) * CH])

        def quant_x(n):
            codes = new(work, "x_codes", n, [P, PASSES * CH], U32)
            scales = new(work, "x_scales", n, [P, PASSES * CH], U8)
            nc.vector.quantize_mx(
                out=codes[:].bitcast(FP8X4),
                scales=scales[:],
                in_=t["x_grp", n][:].rearrange("p a c t -> p (a c t)"),
            )

        def down(n):
            bank = new_bank("z", n, [P, PACK, CH])
            for q in range(PACK):
                for a in range(PASSES):
                    w_cols = slice(q * P, (q + 1) * P)
                    x_cols = slice(a * CH, (a + 1) * CH)
                    nc.tensor.matmul_mx(
                        out=bank[:, q, :],
                        lhsT=wd_codes[:, a, w_cols].bitcast(FP8X4),
                        lhsT_scale=wd_scales[:, a, w_cols],
                        rhs=t["x_codes", n][:, x_cols].bitcast(FP8X4),
                        rhs_scale=t["x_scales", n][:, x_cols],
                        start=(a == 0),
                        stop=(a == PASSES - 1),
                    )

        def gelu(n):
            tile = new(work, "act", n, [P, CH, PACK], F32)
            nc.scalar.activation(out=tile[:], in_=t["z", n][:].rearrange("p t c -> p c t"), func=GELU)

        def scale_h(n):
            tile = new(work, "h", n, [P, CH, PACK], BF16)
            nc.vector.tensor_tensor(out=tile[:], in0=t["act", n][:], in1=scale_bank[:].rearrange("p (c t) -> p c t", t=PACK), op=MULT)

        def quant_h(n):
            g, rest = divmod(n, TILES)
            if rest == 0:
                new(work, "h_codes", g, [P, B * G], U32)
                new(work, "h_scales", g, [P, B * G], U8)
            cols = slice(rest * CH, (rest + 1) * CH)
            nc.vector.quantize_mx(
                out=t["h_codes", g][:, cols].bitcast(FP8X4),
                scales=t["h_scales", g][:, cols],
                in_=t["h", n][:].rearrange("p c t -> p (c t)"),
            )

        def up(k, b):
            g, j = divmod(k, TILES)
            bank = new_bank("u", (k, b), [P, G])
            w_cols = slice(j * P, (j + 1) * P)
            h_cols = slice(b * G, (b + 1) * G)
            nc.tensor.matmul_mx(
                out=bank[:],
                lhsT=wu_codes[:, w_cols].bitcast(FP8X4),
                lhsT_scale=wu_scales[:, w_cols],
                rhs=t["h_codes", g][:, h_cols].bitcast(FP8X4),
                rhs_scale=t["h_scales", g][:, h_cols],
                start=True,
                stop=True,
            )

        def affine(k, b, lo, hi):
            g, j = divmod(k, TILES)
            if ("y", k) not in t:
                new(work, "y", k, [P, B, G], F32)
            nc.vector.scalar_tensor_tensor(
                out=t["y", k][:, b, lo:hi],
                in0=t["u", (k, b)][:, lo:hi],
                scalar=b_col[:, j : j + 1],
                in1=t["gain", g][:, lo:hi],
                op0=ADD,
                op1=MULT,
            )

        def add_r(k, lo, hi, engine):
            y = t["y", k][:, :, lo:hi]
            builder = nc.gpsimd if engine == "pool" else nc.vector
            builder.tensor_tensor(out=y, in0=y, in1=t["r", k][:, :, lo:hi], op=ADD)

        def store_y(k):
            g, j = divmod(k, TILES)
            nc.sync.dma_start(out=out_0[j * P : (j + 1) * P, :, g * G : (g + 1) * G], in_=t["y", k][:])

        def round_y(k, engine):
            tile = new(work, "y16", k, [P, 2, B * P, 2], BF16)
            copy_on(engine, tile[:], t["y", k][:].rearrange("p b d -> p (b d)").rearrange("p (n u e) -> p u n e", u=2, e=2))

        def turn_y(k):
            bank = new_bank("yt", k, [P, PACK, P])
            words = t["y16", k][:].rearrange("p u n e -> p (u n e)").bitcast(F32)
            for b in range(B):
                for u in range(2):
                    first = (u * B + b) * P
                    nc.tensor.transpose(bank[:, 2 * b + u, :], words[:, first : first + P], ident[:])

        def group_y(k, engine):
            tile = new(work, "y_grp", k, [P, P * B * PACK], BF16)
            copy_on(
                engine,
                tile[:].bitcast(F32).rearrange("p (s q) -> p s q", q=PACK),
                t["yt", k][:].rearrange("p q s -> p s q"),
            )

        def quant_y(k):
            g, j = divmod(k, TILES)
            if j == 0:
                new(work, "y_codes", g, [P, S * B], U32)
                new(work, "y_scales", g, [P, S * B], U8)
            cols = slice(j * P * B, (j + 1) * P * B)
            nc.vector.quantize_mx(
                out=t["y_codes", g][:, cols].bitcast(FP8X4), scales=t["y_scales", g][:, cols], in_=t["y_grp", k][:]
            )

        def store_codes(g, lo, hi):
            cols = slice(lo * P * B, hi * P * B)
            words = out_1[g].rearrange("p m t -> p (m t)").bitcast(I32)
            nc.sync.dma_start(out=words[:, cols], in_=t["y_codes", g][:, cols].bitcast(I32))

        def store_scales(g):
            rows = out_2[g].bitcast(I32)
            plane = t["y_scales", g][:].bitcast(I32)
            for q in range(4):
                nc.sync.dma_start(out=rows[4 * q : 4 * q + 4, :], in_=plane[32 * q : 32 * q + 4, :])

        steps = {
            "setup": setup, "load_small": load_small, "spread_scale": spread_scale, "bias_rows": bias_rows,
            "bias_turn": bias_turn, "bias_cols": bias_cols, "load_gain": load_gain, "load_wd": load_wd,
            "load_wu": load_wu, "load_x": load_x, "load_r": load_r, "group_wd": group_wd, "quant_wd": quant_wd,
            "group_wu": group_wu, "quant_wu": quant_wu, "group_x": group_x, "quant_x": quant_x, "down": down,
            "gelu": gelu, "scale_h": scale_h, "quant_h": quant_h, "up": up, "affine": affine, "add_r": add_r,
            "store_y": store_y, "round_y": round_y, "turn_y": turn_y, "group_y": group_y, "quant_y": quant_y,
            "store_codes": store_codes, "store_scales": store_scales,
        }
        for step in program_order():
            steps[step[0]](*step[1:])
